import numpy as np
import ml_dtypes


def mxq(x, axis, fmt="e4m3"):
    dtype, down = {"e4m3": (ml_dtypes.float8_e4m3fn, 7), "e5m2": (ml_dtypes.float8_e5m2, 14)}[fmt]
    v = np.moveaxis(np.asarray(x, np.float32).astype(ml_dtypes.bfloat16).astype(np.float64), axis, -1)
    blocks = v.reshape(v.shape[:-1] + (-1, 32))
    amax = np.abs(blocks).max(-1, keepdims=True)
    byte = np.maximum(np.where(amax > 0, np.frexp(amax)[1] - 1 + 127, 0) - down, 1)
    scale = np.exp2(byte - 127.0)
    codes = (blocks / scale).astype(np.float32).astype(dtype).astype(np.float64)
    return np.moveaxis((codes * scale).reshape(v.shape), -1, axis)


WIDE = False


def mx_kscale(k):
    if not WIDE:
        return np.ones(k)
    levels = np.array([10, -10, 5, -5, 0])
    if k % 512:
        return np.exp2(np.random.permutation(np.resize(levels, k // 32))).repeat(32)
    a = np.empty((k // 512, 16))
    for p in range(k // 512):
        a[p, :8] = np.random.permutation(np.resize(levels, 8))
        for g in range(8):
            far = levels[np.abs(levels - a[p, g]) >= 10]
            a[p, g + 8] = far[np.random.randint(len(far))]
    return np.exp2(a.ravel()).repeat(32)


def f64(x):
    return np.asarray(x).astype(np.float64)


def striped(idx):
    return np.tile(idx.reshape(-1, 16).T, (8, 1)).astype(np.uint16)


def unstriped(offs):
    return offs[:16].T.reshape(-1).astype(np.int64)


def pack_weight(w):
    k, n = w.shape
    w = f64(np.asarray(w, np.float32).astype(ml_dtypes.bfloat16)).reshape(k // 32, 32, n)
    amax = np.abs(w).max(1)
    byte = np.clip(np.where(amax > 0, np.frexp(amax)[1] - 1 + 127 - 7, 1), 1, 254)
    scaled = (w * np.exp2(127.0 - byte)[:, None, :]).reshape(k, n).astype(np.float32)
    words = np.ascontiguousarray(scaled.reshape(k // 512, 128, 4, n).transpose(0, 1, 3, 2)).astype(ml_dtypes.float8_e4m3fn).view(np.uint8)
    return words, np.ascontiguousarray(byte.astype(np.uint8).reshape(k // 512, 16, n))


def unpack_weight(words, scales):
    g, p, n, _ = words.shape
    vals = np.ascontiguousarray(words).view(ml_dtypes.float8_e4m3fn).astype(np.float64) * np.repeat(np.exp2(scales.astype(np.float64) - 127.0), 8, axis=1)[..., None]
    return vals.transpose(0, 1, 3, 2).reshape(g * 512, n)


def relu(v):
    return np.maximum(v, 0.0)


K, T, S, D, N = 512, 2048, 1024, 8, 256
P = 2 ** 7


def setup_inputs():
    n = np.random.standard_normal
    s = mx_kscale(K)[:, None]
    packed_xT = pack_weight(n((K, T)) * s)
    return {
        "x_words": packed_xT[0],
        "x_scales": packed_xT[1],
        "w1": (n((K, N)) / np.sqrt(K) / s).astype(np.float32),
        "w2": (n((K, N)) / np.sqrt(K) / s).astype(np.float32),
        "dist2": (np.tile(np.random.uniform(0.0, 1.2, S), (P, 1))).astype(np.float32),
        "band": (-np.random.uniform(0.8, 1.9, (N, 1))).astype(np.float32),
        "offs": striped(np.random.permutation(T)[:S]),
    }


def reference(x_words, x_scales, w1, w2, dist2, band, offs):
    wt = (relu(f64(band) * f64(dist2)[:1] + 1.3)) ** 2
    xq = unpack_weight(x_words, x_scales)[:, unstriped(offs)]
    yv = mxq(f64(w2), 0, "e4m3").T @ xq
    syj = wt * yv
    sy = syj.reshape(len(syj), -1, D).sum(axis=2)
    s0 = wt.reshape(len(wt), -1, D).sum(axis=2) + 0.2
    my = sy / s0
    xv = mxq(f64(w1), 0, "e4m3").T @ xq
    sxj = wt * xv
    sx = sxj.reshape(len(sxj), -1, D).sum(axis=2)
    mx = sx / s0
    sxyj = (wt * (xv - np.repeat(mx, D, axis=1))) * (yv - np.repeat(my, D, axis=1))
    sxy = sxyj.reshape(len(sxyj), -1, D).sum(axis=2)
    sxxj = wt * ((xv - np.repeat(mx, D, axis=1)) ** 2)
    sxx = sxxj.reshape(len(sxxj), -1, D).sum(axis=2)
    slope = sxy / (sxx + 0.3)
    wr = wt * ((yv - np.repeat(my, D, axis=1) - (np.repeat(slope, D, axis=1) * (xv - np.repeat(mx, D, axis=1)))) ** 2)
    return wr.reshape(len(wr), -1, D).sum(axis=2)

@@ -1,0 +1,209 @@
+from contextlib import ExitStack
+
+import concourse.mybir as mybir
+
+F32 = mybir.dt.float32
+BF16 = mybir.dt.bfloat16
+I32 = mybir.dt.int32
+U32 = mybir.dt.uint32
+U16 = mybir.dt.uint16
+U8 = mybir.dt.uint8
+FP8X4 = mybir.dt.float8_e4m3fn_x4
+ALU = mybir.AluOpType
+ACT = mybir.ActivationFunctionType
+
+K, T, S, D, N = 512, 2048, 1024, 8, 256
+P = 128
+V = S // D
+BLOCKS = N // P
+HALVES = 2
+HALF = S // HALVES
+VH = V // HALVES
+FLOPS = 2 * 2 * K * N * S
+
+
+def tile_picked_ygwrg_rss_p_kernel(tc, x_words, x_scales, w1, w2, dist2, band, offs, out):
+    nc = tc.nc
+    with ExitStack() as ctx:
+        sb = ctx.enter_context(tc.tile_pool(name="sb", bufs=1))
+        ps = ctx.enter_context(tc.psum_pool(name="ps", bufs=1))
+
+        offsets = sb.tile([P, S // 16], U16, name="offsets")
+        nc.sync.dma_start(offsets[:], offs)
+        table_scales = sb.tile([P, T], U8, name="table_scales", align_bytes=64)
+        nc.vector.memset(table_scales[:].bitcast(I32), 0)
+        for q in range(4):
+            nc.scalar.dma_start(table_scales[32 * q : 32 * q + 4, :].bitcast(I32), x_scales[0, 4 * q : 4 * q + 4, :].bitcast(I32))
+        dist = sb.tile([P, D], F32, name="dist")
+        nc.sync.dma_start(dist[:], dist2[0, :].rearrange("(v d) -> v d", d=D))
+        bands = sb.tile([P, BLOCKS], F32, name="bands")
+        with nc.allow_non_contiguous_dma(reason="one value a partition and block"):
+            nc.sync.dma_start(bands[:], band.rearrange("(b p) o -> p (b o)", p=P))
+        raw = [sb.tile([P, 4, N], F32, name="raw0")]
+        nc.sync.dma_start(raw[0][:], w1.rearrange("(p j) n -> p j n", j=4))
+        ident = sb.tile([P, P], F32, name="ident")
+        ones = sb.tile([P, 32], F32, name="ones", tag="table_words", align_bytes=64)
+        count = sb.tile([P, 32], F32, name="count", tag="raw1", align_bytes=64)
+        count_t = sb.tile([P, 32], F32, name="count_t", align_bytes=64)
+        nc.vector.memset(ones[:], 1.0)
+        nc.vector.memset(ident[:], 0.0)
+        nc.vector.tensor_tensor_scan(count[:], ones[:], ones[:], 0.0, ALU.mult, ALU.add)
+        nc.vector.transpose(count_t[:], count[:])
+        for q in range(4):
+            rows = slice(32 * q, 32 * (q + 1))
+            nc.vector.tensor_tensor(ident[rows, rows], count[rows, :], count_t[rows, :], ALU.is_equal)
+
+        table_words = sb.tile([P, T], I32, name="table_words", tag="table_words", align_bytes=64)
+        nc.sync.dma_start(table_words[:], x_words[0].rearrange("p c r -> p (c r)").bitcast(I32))
+
+        raw.append(sb.tile([P, 4, N], F32, name="raw1", tag="raw1", align_bytes=64))
+        nc.sync.dma_start(raw[1][:], w2.rearrange("(p j) n -> p j n", j=4))
+
+        def tsum(dst, parts):
+            for i, part in enumerate(parts):
+                nc.tensor.matmul(dst, lhsT=part, rhs=ident[:], start=(i == 0), stop=(i == len(parts) - 1), is_transpose=True)
+
+        def dsum(dst, tile):
+            tsum(dst, [tile[:, d, :] for d in range(D)])
+
+        def wide(name):
+            return [sb.tile([P, D, V], F32, name="%s%d" % (name, b)) for b in range(BLOCKS)]
+
+        def small(name):
+            return sb.tile([P, N], F32, name=name)
+
+        def half(tile, h):
+            return tile[:, :, VH * h : VH * (h + 1)]
+
+        def dhalf(tile, i):
+            return tile[:, 4 * i : 4 * (i + 1), :]
+
+        picked_scales = [sb.tile([P, HALF], U8, name="picked_scales%d" % h, align_bytes=64) for h in range(HALVES)]
+        picked_words = [sb.tile([P, HALF], U32, name="picked_words%d" % h, align_bytes=64) for h in range(HALVES)]
+
+        def lst(h):
+            return offsets[:, h * HALF // 16 : (h + 1) * HALF // 16]
+
+        for h in range(HALVES):
+            nc.vector.tensor_copy(picked_scales[h][:], table_scales[:].indirect(lst(h)))
+
+        spread = [ps.tile([P, 4, V], F32, name="spread%d" % i, tag="mm%d" % i) for i in range(2)]
+        for d in range(D):
+            nc.tensor.transpose(spread[d // 4][:, d % 4, :], dist[:, d : d + 1].to_broadcast([P, P]), ident[:])
+        root = wide("root")
+        wt = wide("wt")
+        for b in range(BLOCKS):
+            for i in range(2):
+                nc.scalar.activation(dhalf(root[b], i), spread[i][:], ACT.Relu, bias=1.3, scale=bands[:, b : b + 1])
+
+        codes = [sb.tile([P, N], U32, name="codes%d" % i, align_bytes=64) for i in range(2)]
+        scales = [sb.tile([P, N], U8, name="scales%d" % i, align_bytes=64) for i in range(2)]
+        grouped = [sb.tile([P, N, 4], BF16, name="grouped%d" % i, align_bytes=64) for i in range(2)]
+
+        def weave(i):
+            return grouped[i][:].rearrange("p (c i) t -> p c t i", i=4), raw[i][:].rearrange("p t (c i) -> p c t i", i=4)
+
+        def quantize(i):
+            nc.vector.quantize_mx(out=codes[i][:].bitcast(FP8X4), scales=scales[i][:], in_=grouped[i][:].rearrange("p n t -> p (n t)"))
+
+        nc.vector.tensor_copy(*weave(0))
+        quantize(0)
+        for h in range(HALVES):
+            nc.vector.tensor_copy(picked_words[h][:], table_words[:].bitcast(U32).indirect(lst(h)))
+
+        for b in range(BLOCKS):
+            for i in range(2):
+                nc.scalar.activation(dhalf(wt[b], i), dhalf(root[b], i), ACT.Square)
+        nc.scalar.copy(*weave(1))
+
+        third = ps.tile([P, N], F32, name="wsum", tag="sum2")
+        for b in range(BLOCKS):
+            dsum(third[:, P * b : P * (b + 1)], wt[b])
+
+        def product(i, b, h, slot):
+            bank = ps.tile([P, HALF], F32, name="bank", tag="mm%d" % slot)
+            cols = slice(P * b, P * (b + 1))
+            nc.tensor.matmul_mx(out=bank[:], lhsT=codes[i][:, cols].bitcast(FP8X4), lhsT_scale=scales[i][:, cols],
+                                rhs=picked_words[h][:].bitcast(FP8X4), rhs_scale=picked_scales[h][:], start=True, stop=True)
+            return bank[:].rearrange("p (v d) -> p d v", d=D)
+
+        def inverse_form(src, shift, slope, name):
+            rs, r, f, res = small(name + "_rs"), small(name + "_r"), small(name + "_f"), small(name)
+            nc.scalar.activation(rs[:], src, ACT.Abs_reciprocal_sqrt, bias=shift)
+            nc.scalar.activation(r[:], rs[:], ACT.Square)
+            nc.gpsimd.tensor_scalar(f[:], r[:], slope, 1.0, ALU.mult, ALU.add)
+            nc.gpsimd.tensor_tensor(res[:], r[:], f[:], ALU.mult)
+            return res
+
+        u, wx, uu = wide("u"), wide("wx"), wide("uu")
+        t, wy, tt, ut = wide("t"), wide("wy"), wide("tt"), wide("ut")
+        xs = [[product(0, b, h, 2 * h + b) for b in range(BLOCKS)] for h in range(HALVES)]
+        centre = inverse_form(third[:], 0.2, 0.2, "centre")
+
+        for h in range(HALVES):
+            nc.vector.tensor_tensor(half(u[0], h), xs[h][0], half(root[0], h), ALU.mult)
+            nc.gpsimd.tensor_tensor(half(wx[0], h), half(u[0], h), half(root[0], h), ALU.mult)
+        quantize(1)
+        for h in range(HALVES):
+            nc.vector.tensor_tensor(half(u[1], h), xs[h][1], half(root[1], h), ALU.mult)
+        for h in range(HALVES):
+            nc.vector.tensor_tensor(half(wx[1], h), xs[h][1], half(wt[1], h), ALU.mult)
+        ys0 = [product(1, 0, h, (4, 0)[h]) for h in range(HALVES)]
+        sum_x = ps.tile([P, 2, N], F32, name="sum_x", tag="sum0")
+        sum_y = ps.tile([P, 2, N], F32, name="sum_y", tag="sum1")
+        sum_xy = ps.tile([P, N], F32, name="sum_xy", tag="sum2")
+        for b in range(BLOCKS):
+            for i in range(2):
+                nc.scalar.activation(dhalf(uu[b], i), dhalf(u[b], i), ACT.Square)
+        dsum(sum_x[:, 1, 0:P], uu[0])
+        ys1 = [product(1, 1, h, (2, 1)[h]) for h in range(HALVES)]
+        dsum(sum_x[:, 0, 0:P], wx[0])
+        dsum(sum_x[:, 1, P:N], uu[1])
+        dsum(sum_x[:, 0, P:N], wx[1])
+
+        for h in range(HALVES):
+            nc.vector.tensor_tensor(half(t[0], h), ys0[h], half(root[0], h), ALU.mult)
+        for i in range(2):
+            nc.gpsimd.tensor_tensor(dhalf(ut[0], i), dhalf(u[0], i), dhalf(t[0], i), ALU.mult)
+            nc.scalar.activation(dhalf(tt[0], i), dhalf(t[0], i), ACT.Square)
+        for h in range(HALVES):
+            nc.vector.tensor_tensor(half(wy[0], h), ys0[h], half(wt[0], h), ALU.mult)
+        csx, csxx, den = small("csx"), small("csxx"), small("den")
+        nc.vector.tensor_tensor(csx[:], sum_x[:, 0, :], centre[:], ALU.mult)
+        for h in range(HALVES):
+            nc.vector.tensor_tensor(half(wy[1], h), ys1[h], half(wt[1], h), ALU.mult)
+            if h == 0:
+                nc.vector.tensor_tensor(csxx[:], sum_x[:, 0, :], csx[:], ALU.mult)
+        nc.vector.tensor_tensor(den[:], sum_x[:, 1, :], csxx[:], ALU.subtract)
+        dsum(sum_y[:, 1, 0:P], tt[0])
+        dsum(sum_y[:, 0, 0:P], wy[0])
+        dsum(sum_xy[:, 0:P], ut[0])
+        dsum(sum_y[:, 0, P:N], wy[1])
+        for h in range(HALVES):
+            nc.vector.tensor_tensor(half(t[1], h), ys1[h], half(root[1], h), ALU.mult)
+        nc.gpsimd.tensor_tensor(half(ut[1], 0), half(u[1], 0), half(t[1], 0), ALU.mult)
+        gain = inverse_form(den[:], 0.3, 0.3, "gain")
+        nc.vector.tensor_tensor(half(ut[1], 1), ys1[1], half(wx[1], 1), ALU.mult)
+        csxy, sy2, csyy, nsyy = small("csxy"), small("sy2"), small("csyy"), small("nsyy")
+        nc.vector.tensor_tensor(csxy[:], sum_y[:, 0, :], csx[:], ALU.mult)
+        nc.scalar.activation(sy2[:], sum_y[:, 0, :], ACT.Square)
+        for i in range(2):
+            nc.scalar.activation(dhalf(tt[1], i), dhalf(t[1], i), ACT.Square)
+        nc.gpsimd.tensor_tensor(csyy[:], sy2[:], centre[:], ALU.mult)
+        dsum(sum_xy[:, P:N], ut[1])
+        dsum(sum_y[:, 1, P:N], tt[1])
+        nc.scalar.activation(nsyy[:], sum_y[:, 1, :], ACT.Copy, scale=-1.0)
+        xy, kxy, fit = small("xy"), small("kxy"), small("fit")
+        nc.vector.tensor_tensor(xy[:], sum_xy[:], csxy[:], ALU.subtract)
+        nc.vector.tensor_tensor(kxy[:], xy[:], gain[:], ALU.mult)
+        nc.vector.tensor_tensor(fit[:], kxy[:], xy[:], ALU.mult)
+        for b in range(BLOCKS):
+            cols = slice(P * b, P * (b + 1))
+            turned = ps.tile([P, V], F32, name="turned", tag="mm%d" % (3 + b))
+            tsum(turned[:], [csyy[:, cols], nsyy[:, cols], fit[:, cols]])
+            res = sb.tile([P, V], F32, name="res%d" % b)
+            if b == 0:
+                nc.scalar.activation(res[:], turned[:], ACT.Copy, scale=-1.0)
+            else:
+                nc.vector.tensor_scalar(res[:], turned[:], -1.0, None, ALU.mult)
+            nc.sync.dma_start(out[cols, :], res[:])

@@ -11,6 +11,7 @@ U8 = mybir.dt.uint8
 FP8X4 = mybir.dt.float8_e4m3fn_x4
 ALU = mybir.AluOpType
 ACT = mybir.ActivationFunctionType
+AX = mybir.AxisListType
 
 K, T, S, D, N = 512, 2048, 1024, 8, 256
 P = 128
@@ -30,21 +31,22 @@ def tile_picked_ygwrg_rss_p_kernel(tc, x_words, x_scales, w1, w2, dist2, band, o
 
         offsets = sb.tile([P, S // 16], U16, name="offsets")
         nc.sync.dma_start(offsets[:], offs)
+        dist = sb.tile([P, D], F32, name="dist")
+        nc.scalar.dma_start(dist[:], dist2[0, :].rearrange("(v d) -> v d", d=D))
+        bands = sb.tile([P, BLOCKS], F32, name="bands", tag="grouped1", align_bytes=64)
+        with nc.allow_non_contiguous_dma(reason="one value a partition and block"):
+            nc.scalar.dma_start(bands[:], band.rearrange("(b p) o -> p (b o)", p=P))
         table_scales = sb.tile([P, T], U8, name="table_scales", align_bytes=64)
         nc.vector.memset(table_scales[:].bitcast(I32), 0)
         for q in range(4):
-            nc.scalar.dma_start(table_scales[32 * q : 32 * q + 4, :].bitcast(I32), x_scales[0, 4 * q : 4 * q + 4, :].bitcast(I32))
-        dist = sb.tile([P, D], F32, name="dist")
-        nc.sync.dma_start(dist[:], dist2[0, :].rearrange("(v d) -> v d", d=D))
-        bands = sb.tile([P, BLOCKS], F32, name="bands")
-        with nc.allow_non_contiguous_dma(reason="one value a partition and block"):
-            nc.sync.dma_start(bands[:], band.rearrange("(b p) o -> p (b o)", p=P))
-        raw = [sb.tile([P, 4, N], F32, name="raw0")]
-        nc.sync.dma_start(raw[0][:], w1.rearrange("(p j) n -> p j n", j=4))
+            (nc.sync, nc.scalar)[q % 2].dma_start(table_scales[32 * q : 32 * q + 4, :].bitcast(I32), x_scales[0, 4 * q : 4 * q + 4, :].bitcast(I32))
+        warm = sb.tile([P, 2], F32, name="warm")
+        nc.vector.memset(warm[:, 0:1], 1.0)
+        nc.scalar.activation(warm[:, 1:2], warm[:, 0:1], ACT.Abs_reciprocal_sqrt)
         ident = sb.tile([P, P], F32, name="ident")
         ones = sb.tile([P, 32], F32, name="ones", tag="table_words", align_bytes=64)
-        count = sb.tile([P, 32], F32, name="count", tag="raw1", align_bytes=64)
-        count_t = sb.tile([P, 32], F32, name="count_t", align_bytes=64)
+        count = sb.tile([P, 32], F32, name="count", tag="raw0", align_bytes=64)
+        count_t = sb.tile([P, 32], F32, name="count_t", tag="raw1", align_bytes=64)
         nc.vector.memset(ones[:], 1.0)
         nc.vector.memset(ident[:], 0.0)
         nc.vector.tensor_tensor_scan(count[:], ones[:], ones[:], 0.0, ALU.mult, ALU.add)
@@ -56,8 +58,9 @@ def tile_picked_ygwrg_rss_p_kernel(tc, x_words, x_scales, w1, w2, dist2, band, o
         table_words = sb.tile([P, T], I32, name="table_words", tag="table_words", align_bytes=64)
         nc.sync.dma_start(table_words[:], x_words[0].rearrange("p c r -> p (c r)").bitcast(I32))
 
-        raw.append(sb.tile([P, 4, N], F32, name="raw1", tag="raw1", align_bytes=64))
-        nc.sync.dma_start(raw[1][:], w2.rearrange("(p j) n -> p j n", j=4))
+        raw = [sb.tile([P, 4, N], F32, name="raw%d" % i, tag="raw%d" % i, align_bytes=64) for i in range(2)]
+        for i, w in enumerate((w1, w2)):
+            nc.sync.dma_start(raw[i][:], w.rearrange("(p j) n -> p j n", j=4))
 
         def tsum(dst, parts):
             for i, part in enumerate(parts):
@@ -79,7 +82,7 @@ def tile_picked_ygwrg_rss_p_kernel(tc, x_words, x_scales, w1, w2, dist2, band, o
             return tile[:, 4 * i : 4 * (i + 1), :]
 
         picked_scales = [sb.tile([P, HALF], U8, name="picked_scales%d" % h, align_bytes=64) for h in range(HALVES)]
-        picked_words = [sb.tile([P, HALF], U32, name="picked_words%d" % h, align_bytes=64) for h in range(HALVES)]
+        picked_words = [sb.tile([P, HALF], U32, name="picked_words0", align_bytes=64)]
 
         def lst(h):
             return offsets[:, h * HALF // 16 : (h + 1) * HALF // 16]
@@ -87,18 +90,13 @@ def tile_picked_ygwrg_rss_p_kernel(tc, x_words, x_scales, w1, w2, dist2, band, o
         for h in range(HALVES):
             nc.vector.tensor_copy(picked_scales[h][:], table_scales[:].indirect(lst(h)))
 
-        spread = [ps.tile([P, 4, V], F32, name="spread%d" % i, tag="mm%d" % i) for i in range(2)]
+        spread = [ps.tile([P, 4, V], F32, name="spread%d" % i, tag="sum%d" % i) for i in range(2)]
         for d in range(D):
             nc.tensor.transpose(spread[d // 4][:, d % 4, :], dist[:, d : d + 1].to_broadcast([P, P]), ident[:])
         root = wide("root")
-        wt = wide("wt")
-        for b in range(BLOCKS):
-            for i in range(2):
-                nc.scalar.activation(dhalf(root[b], i), spread[i][:], ACT.Relu, bias=1.3, scale=bands[:, b : b + 1])
-
         codes = [sb.tile([P, N], U32, name="codes%d" % i, align_bytes=64) for i in range(2)]
         scales = [sb.tile([P, N], U8, name="scales%d" % i, align_bytes=64) for i in range(2)]
-        grouped = [sb.tile([P, N, 4], BF16, name="grouped%d" % i, align_bytes=64) for i in range(2)]
+        grouped = [sb.tile([P, N, 4], BF16, name="grouped%d" % i, tag="grouped%d" % i, align_bytes=64) for i in range(2)]
 
         def weave(i):
             return grouped[i][:].rearrange("p (c i) t -> p c t i", i=4), raw[i][:].rearrange("p t (c i) -> p c t i", i=4)
@@ -106,19 +104,21 @@ def tile_picked_ygwrg_rss_p_kernel(tc, x_words, x_scales, w1, w2, dist2, band, o
         def quantize(i):
             nc.vector.quantize_mx(out=codes[i][:].bitcast(FP8X4), scales=scales[i][:], in_=grouped[i][:].rearrange("p n t -> p (n t)"))
 
-        nc.vector.tensor_copy(*weave(0))
-        quantize(0)
-        for h in range(HALVES):
-            nc.vector.tensor_copy(picked_words[h][:], table_words[:].bitcast(U32).indirect(lst(h)))
-
-        for b in range(BLOCKS):
-            for i in range(2):
-                nc.scalar.activation(dhalf(wt[b], i), dhalf(root[b], i), ACT.Square)
-        nc.scalar.copy(*weave(1))
-
+        wt = []
         third = ps.tile([P, N], F32, name="wsum", tag="sum2")
         for b in range(BLOCKS):
-            dsum(third[:, P * b : P * (b + 1)], wt[b])
+            for i in range(2):
+                nc.scalar.activation(dhalf(root[b], i), spread[i][:], ACT.Relu, bias=1.3, scale=bands[:, b : b + 1])
+            if b == 1:
+                nc.scalar.copy(*weave(1))
+            wt.append(sb.tile([P, D, V], F32, name="wt%d" % b, tag=("wt0", "raw1")[b], align_bytes=64))
+            for i in range(2):
+                nc.scalar.activation(dhalf(wt[b], i), dhalf(root[b], i), ACT.Square)
+        nc.vector.tensor_copy(picked_words[0][:], table_words[:].bitcast(U32).indirect(lst(0)))
+        nc.vector.tensor_copy(*weave(0))
+        quantize(0)
+        picked_words.append(sb.tile([P, HALF], U32, name="picked_words1", tag="grouped0", align_bytes=64))
+        nc.vector.tensor_copy(picked_words[1][:], table_words[:].bitcast(U32).indirect(lst(1)))
 
         def product(i, b, h, slot):
             bank = ps.tile([P, HALF], F32, name="bank", tag="mm%d" % slot)
@@ -127,83 +127,108 @@ def tile_picked_ygwrg_rss_p_kernel(tc, x_words, x_scales, w1, w2, dist2, band, o
                                 rhs=picked_words[h][:].bitcast(FP8X4), rhs_scale=picked_scales[h][:], start=True, stop=True)
             return bank[:].rearrange("p (v d) -> p d v", d=D)
 
-        def inverse_form(src, shift, slope, name):
-            rs, r, f, res = small(name + "_rs"), small(name + "_r"), small(name + "_f"), small(name)
+        def inverse_form(src, shift, name):
+            rs, r, f = small(name + "_rs"), small(name + "_r"), small(name + "_f")
             nc.scalar.activation(rs[:], src, ACT.Abs_reciprocal_sqrt, bias=shift)
             nc.scalar.activation(r[:], rs[:], ACT.Square)
-            nc.gpsimd.tensor_scalar(f[:], r[:], slope, 1.0, ALU.mult, ALU.add)
-            nc.gpsimd.tensor_tensor(res[:], r[:], f[:], ALU.mult)
+            nc.scalar.activation(f[:], r[:], ACT.Square)
+            return f
+
+        def squares(dst, src):
+            for i in range(2):
+                nc.scalar.activation(dhalf(dst, i), dhalf(src, i), ACT.Square)
+
+        def mul(dst, bank, factor, h):
+            nc.vector.tensor_tensor(half(dst, h), bank, half(factor, h), ALU.mult)
+
+        uu, u = wide("uu"), wide("u")
+        t, wy, tt, ut = wide("t"), wide("wy"), wide("tt"), wide("ut")
+        def both(name, in0, in1, op):
+            res = small(name)
+            nc.vector.tensor_tensor(res[:], in0, in1, op)
             return res
 
-        u, wx, uu = wide("u"), wide("wx"), wide("uu")
-        t, wy, tt, ut = wide("t"), wide("wy"), wide("tt"), wide("ut")
-        xs = [[product(0, b, h, 2 * h + b) for b in range(BLOCKS)] for h in range(HALVES)]
-        centre = inverse_form(third[:], 0.2, 0.2, "centre")
+        def shifted(name, src, shift, r2):
+            res = small(name)
+            nc.vector.scalar_tensor_tensor(res[:], src, shift, r2[:], ALU.add, ALU.mult)
+            return res
 
-        for h in range(HALVES):
-            nc.vector.tensor_tensor(half(u[0], h), xs[h][0], half(root[0], h), ALU.mult)
-            nc.gpsimd.tensor_tensor(half(wx[0], h), half(u[0], h), half(root[0], h), ALU.mult)
+        def pool_mul(dst, in0, in1):
+            nc.gpsimd.tensor_tensor(dst, in0, in1, ALU.mult)
+
+        dsum(third[:, 0:P], wt[0])
+        x00, x10 = product(0, 0, 0, 0), product(0, 1, 0, 1)
+        x01, x11 = product(0, 0, 1, 2), product(0, 1, 1, 3)
         quantize(1)
-        for h in range(HALVES):
-            nc.vector.tensor_tensor(half(u[1], h), xs[h][1], half(root[1], h), ALU.mult)
-        for h in range(HALVES):
-            nc.vector.tensor_tensor(half(wx[1], h), xs[h][1], half(wt[1], h), ALU.mult)
-        ys0 = [product(1, 0, h, (4, 0)[h]) for h in range(HALVES)]
+        wx = [sb.tile([P, D, V], F32, name="wx%d" % b, tag=("grouped1", "wx1")[b], align_bytes=64) for b in range(BLOCKS)]
+        dsum(third[:, P:N], wt[1])
         sum_x = ps.tile([P, 2, N], F32, name="sum_x", tag="sum0")
-        sum_y = ps.tile([P, 2, N], F32, name="sum_y", tag="sum1")
-        sum_xy = ps.tile([P, N], F32, name="sum_xy", tag="sum2")
-        for b in range(BLOCKS):
-            for i in range(2):
-                nc.scalar.activation(dhalf(uu[b], i), dhalf(u[b], i), ACT.Square)
+        sum_y = ps.tile([P, N], F32, name="sum_y", tag="sum1")
+        sum_yy = ps.tile([P, N], F32, name="sum_yy", tag="mm4")
+        for h, bank in enumerate((x00, x01)):
+            mul(u[0], bank, root[0], h)
+            pool_mul(half(wx[0], h), half(u[0], h), half(root[0], h))
+        y00 = product(1, 0, 0, 0)
+        squares(uu[0], u[0])
+        mul(u[1], x10, root[1], 0)
+        mul(u[1], x11, root[1], 1)
+        centre_r2 = inverse_form(third[:], 0.2, "centre")
+        squares(uu[1], u[1])
+        mul(wx[1], x10, wt[1], 0)
+        y01 = product(1, 0, 1, 2)
         dsum(sum_x[:, 1, 0:P], uu[0])
-        ys1 = [product(1, 1, h, (2, 1)[h]) for h in range(HALVES)]
-        dsum(sum_x[:, 0, 0:P], wx[0])
-        dsum(sum_x[:, 1, P:N], uu[1])
+        mul(wx[1], x11, wt[1], 1)
         dsum(sum_x[:, 0, P:N], wx[1])
-
-        for h in range(HALVES):
-            nc.vector.tensor_tensor(half(t[0], h), ys0[h], half(root[0], h), ALU.mult)
+        mul(t[0], y00, root[0], 0)
+        pool_mul(half(wy[0], 0), half(t[0], 0), half(root[0], 0))
+        y10 = product(1, 1, 0, 1)
+        dsum(sum_x[:, 1, P:N], uu[1])
+        dsum(sum_x[:, 0, 0:P], wx[0])
+        mul(t[0], y01, root[0], 1)
         for i in range(2):
-            nc.gpsimd.tensor_tensor(dhalf(ut[0], i), dhalf(u[0], i), dhalf(t[0], i), ALU.mult)
-            nc.scalar.activation(dhalf(tt[0], i), dhalf(t[0], i), ACT.Square)
-        for h in range(HALVES):
-            nc.vector.tensor_tensor(half(wy[0], h), ys0[h], half(wt[0], h), ALU.mult)
-        csx, csxx, den = small("csx"), small("csxx"), small("den")
-        nc.vector.tensor_tensor(csx[:], sum_x[:, 0, :], centre[:], ALU.mult)
-        for h in range(HALVES):
-            nc.vector.tensor_tensor(half(wy[1], h), ys1[h], half(wt[1], h), ALU.mult)
-            if h == 0:
-                nc.vector.tensor_tensor(csxx[:], sum_x[:, 0, :], csx[:], ALU.mult)
-        nc.vector.tensor_tensor(den[:], sum_x[:, 1, :], csxx[:], ALU.subtract)
-        dsum(sum_y[:, 1, 0:P], tt[0])
-        dsum(sum_y[:, 0, 0:P], wy[0])
+            pool_mul(dhalf(ut[0], i), dhalf(u[0], i), dhalf(t[0], i))
+        squares(tt[0], t[0])
+        mul(wy[0], y01, wt[0], 1)
+        y11 = product(1, 1, 1, 2)
+        centre = shifted("centre", third[:], 0.4, centre_r2)
+        sum_xy = ps.tile([P, N], F32, name="sum_xy", tag="sum2")
+        dsum(sum_yy[:, 0:P], tt[0])
+        dsum(sum_y[:, 0:P], wy[0])
+        mul(t[1], y10, root[1], 0)
+        pool_mul(half(ut[1], 0), half(u[1], 0), half(t[1], 0))
+        csx = both("csx", sum_x[:, 0, :], centre[:], ALU.mult)
+        mul(wy[1], y10, wt[1], 0)
+        csxx = both("csxx", sum_x[:, 0, :], csx[:], ALU.mult)
+        mul(wy[1], y11, wt[1], 1)
+        den = both("den", sum_x[:, 1, :], csxx[:], ALU.subtract)
+        gain_r2 = inverse_form(den[:], 0.3, "gain")
+        mul(t[1], y11, root[1], 1)
+        squares(tt[1], t[1])
+        dsum(sum_y[:, P:N], wy[1])
         dsum(sum_xy[:, 0:P], ut[0])
-        dsum(sum_y[:, 0, P:N], wy[1])
-        for h in range(HALVES):
-            nc.vector.tensor_tensor(half(t[1], h), ys1[h], half(root[1], h), ALU.mult)
-        nc.gpsimd.tensor_tensor(half(ut[1], 0), half(u[1], 0), half(t[1], 0), ALU.mult)
-        gain = inverse_form(den[:], 0.3, 0.3, "gain")
-        nc.vector.tensor_tensor(half(ut[1], 1), ys1[1], half(wx[1], 1), ALU.mult)
-        csxy, sy2, csyy, nsyy = small("csxy"), small("sy2"), small("csyy"), small("nsyy")
-        nc.vector.tensor_tensor(csxy[:], sum_y[:, 0, :], csx[:], ALU.mult)
-        nc.scalar.activation(sy2[:], sum_y[:, 0, :], ACT.Square)
         for i in range(2):
-            nc.scalar.activation(dhalf(tt[1], i), dhalf(t[1], i), ACT.Square)
-        nc.gpsimd.tensor_tensor(csyy[:], sy2[:], centre[:], ALU.mult)
+            nc.vector.tensor_tensor(half(dhalf(ut[1], i), 1), y11[:, 4 * i : 4 * (i + 1), :], half(dhalf(wx[1], i), 1), ALU.mult)
         dsum(sum_xy[:, P:N], ut[1])
-        dsum(sum_y[:, 1, P:N], tt[1])
-        nc.scalar.activation(nsyy[:], sum_y[:, 1, :], ACT.Copy, scale=-1.0)
-        xy, kxy, fit = small("xy"), small("kxy"), small("fit")
-        nc.vector.tensor_tensor(xy[:], sum_xy[:], csxy[:], ALU.subtract)
-        nc.vector.tensor_tensor(kxy[:], xy[:], gain[:], ALU.mult)
-        nc.vector.tensor_tensor(fit[:], kxy[:], xy[:], ALU.mult)
-        for b in range(BLOCKS):
-            cols = slice(P * b, P * (b + 1))
-            turned = ps.tile([P, V], F32, name="turned", tag="mm%d" % (3 + b))
-            tsum(turned[:], [csyy[:, cols], nsyy[:, cols], fit[:, cols]])
-            res = sb.tile([P, V], F32, name="res%d" % b)
-            if b == 0:
-                nc.scalar.activation(res[:], turned[:], ACT.Copy, scale=-1.0)
-            else:
-                nc.vector.tensor_scalar(res[:], turned[:], -1.0, None, ALU.mult)
-            nc.sync.dma_start(out[cols, :], res[:])
+        csxy = both("csxy", sum_y[:], csx[:], ALU.mult)
+        sy2 = small("sy2")
+        nc.scalar.activation(sy2[:], sum_y[:], ACT.Square)
+        dsum(sum_yy[:, P:N], tt[1])
+        nsyy = small("nsyy")
+        nc.scalar.activation(nsyy[:], sum_yy[:], ACT.Copy, scale=-1.0)
+        gain = shifted("gain", den[:], 0.6, gain_r2)
+        xy = both("xy", sum_xy[:], csxy[:], ALU.subtract)
+        csyy = both("csyy", sy2[:], centre[:], ALU.mult)
+        kxy = both("kxy", xy[:], gain[:], ALU.mult)
+        fit = both("fit", kxy[:], xy[:], ALU.mult)
+        turned = [ps.tile([P, V], F32, name="turned%d" % b, tag="mm%d" % (0, 2)[b]) for b in range(BLOCKS)]
+        res = [sb.tile([P, V], F32, name="res%d" % b) for b in range(BLOCKS)]
+        parts = [[nsyy[:, 0:P], csyy[:, 0:P], fit[:, 0:P]], [nsyy[:, P:N], csyy[:, P:N], fit[:, P:N]]]
+        for last in (False, True):
+            for b in range(BLOCKS):
+                for i, part in enumerate(parts[b]):
+                    if (i == len(parts[b]) - 1) == last:
+                        nc.tensor.matmul(turned[b][:], lhsT=part, rhs=ident[:], start=(i == 0), stop=last, is_transpose=True)
+        nc.scalar.activation(res[0][:], turned[0][:], ACT.Copy, scale=-1.0)
+        nc.scalar.dma_start(out[0:P, :], res[0][:])
+        nc.vector.tensor_scalar(res[1][:], turned[1][:], -1.0, None, ALU.mult)
+        nc.sync.dma_start(out[P:N, :], res[1][:])

from contextlib import ExitStack

import concourse.mybir as mybir

F32 = mybir.dt.float32
BF16 = mybir.dt.bfloat16
I32 = mybir.dt.int32
U32 = mybir.dt.uint32
U16 = mybir.dt.uint16
U8 = mybir.dt.uint8
FP8X4 = mybir.dt.float8_e4m3fn_x4
ALU = mybir.AluOpType
ACT = mybir.ActivationFunctionType
AX = mybir.AxisListType

K, T, S, D, N = 512, 2048, 1024, 8, 256
P = 128
V = S // D
BLOCKS = N // P
HALVES = 2
HALF = S // HALVES
VH = V // HALVES
FLOPS = 2 * 2 * K * N * S


def tile_picked_ygwrg_rss_p_kernel(tc, x_words, x_scales, w1, w2, dist2, band, offs, out):
    nc = tc.nc
    with ExitStack() as ctx:
        sb = ctx.enter_context(tc.tile_pool(name="sb", bufs=1))
        ps = ctx.enter_context(tc.psum_pool(name="ps", bufs=1))

        offsets = sb.tile([P, S // 16], U16, name="offsets")
        nc.sync.dma_start(offsets[:], offs)
        dist = sb.tile([P, D], F32, name="dist")
        nc.scalar.dma_start(dist[:], dist2[0, :].rearrange("(v d) -> v d", d=D))
        bands = sb.tile([P, BLOCKS], F32, name="bands", tag="grouped1", align_bytes=64)
        with nc.allow_non_contiguous_dma(reason="one value a partition and block"):
            nc.scalar.dma_start(bands[:], band.rearrange("(b p) o -> p (b o)", p=P))
        table_scales = sb.tile([P, T], U8, name="table_scales", align_bytes=64)
        nc.vector.memset(table_scales[:].bitcast(I32), 0)
        for q in range(4):
            (nc.sync, nc.scalar)[q % 2].dma_start(table_scales[32 * q : 32 * q + 4, :].bitcast(I32), x_scales[0, 4 * q : 4 * q + 4, :].bitcast(I32))
        warm = sb.tile([P, 2], F32, name="warm")
        nc.vector.memset(warm[:, 0:1], 1.0)
        nc.scalar.activation(warm[:, 1:2], warm[:, 0:1], ACT.Abs_reciprocal_sqrt)
        ident = sb.tile([P, P], F32, name="ident")
        ones = sb.tile([P, 32], F32, name="ones", tag="table_words", align_bytes=64)
        count = sb.tile([P, 32], F32, name="count", tag="raw0", align_bytes=64)
        count_t = sb.tile([P, 32], F32, name="count_t", tag="raw1", align_bytes=64)
        nc.vector.memset(ones[:], 1.0)
        nc.vector.memset(ident[:], 0.0)
        nc.vector.tensor_tensor_scan(count[:], ones[:], ones[:], 0.0, ALU.mult, ALU.add)
        nc.vector.transpose(count_t[:], count[:])
        for q in range(4):
            rows = slice(32 * q, 32 * (q + 1))
            nc.vector.tensor_tensor(ident[rows, rows], count[rows, :], count_t[rows, :], ALU.is_equal)

        table_words = sb.tile([P, T], I32, name="table_words", tag="table_words", align_bytes=64)
        nc.sync.dma_start(table_words[:], x_words[0].rearrange("p c r -> p (c r)").bitcast(I32))

        raw = [sb.tile([P, 4, N], F32, name="raw%d" % i, tag="raw%d" % i, align_bytes=64) for i in range(2)]
        for i, w in enumerate((w1, w2)):
            nc.sync.dma_start(raw[i][:], w.rearrange("(p j) n -> p j n", j=4))

        def tsum(dst, parts):
            for i, part in enumerate(parts):
                nc.tensor.matmul(dst, lhsT=part, rhs=ident[:], start=(i == 0), stop=(i == len(parts) - 1), is_transpose=True)

        def dsum(dst, tile):
            tsum(dst, [tile[:, d, :] for d in range(D)])

        def wide(name):
            return [sb.tile([P, D, V], F32, name="%s%d" % (name, b)) for b in range(BLOCKS)]

        def small(name):
            return sb.tile([P, N], F32, name=name)

        def half(tile, h):
            return tile[:, :, VH * h : VH * (h + 1)]

        def dhalf(tile, i):
            return tile[:, 4 * i : 4 * (i + 1), :]

        picked_scales = [sb.tile([P, HALF], U8, name="picked_scales%d" % h, align_bytes=64) for h in range(HALVES)]
        picked_words = [sb.tile([P, HALF], U32, name="picked_words0", align_bytes=64)]

        def lst(h):
            return offsets[:, h * HALF // 16 : (h + 1) * HALF // 16]

        for h in range(HALVES):
            nc.vector.tensor_copy(picked_scales[h][:], table_scales[:].indirect(lst(h)))

        spread = [ps.tile([P, 4, V], F32, name="spread%d" % i, tag="sum%d" % i) for i in range(2)]
        for d in range(D):
            nc.tensor.transpose(spread[d // 4][:, d % 4, :], dist[:, d : d + 1].to_broadcast([P, P]), ident[:])
        root = wide("root")
        codes = [sb.tile([P, N], U32, name="codes%d" % i, align_bytes=64) for i in range(2)]
        scales = [sb.tile([P, N], U8, name="scales%d" % i, align_bytes=64) for i in range(2)]
        grouped = [sb.tile([P, N, 4], BF16, name="grouped%d" % i, tag="grouped%d" % i, align_bytes=64) for i in range(2)]

        def weave(i):
            return grouped[i][:].rearrange("p (c i) t -> p c t i", i=4), raw[i][:].rearrange("p t (c i) -> p c t i", i=4)

        def quantize(i):
            nc.vector.quantize_mx(out=codes[i][:].bitcast(FP8X4), scales=scales[i][:], in_=grouped[i][:].rearrange("p n t -> p (n t)"))

        wt = []
        third = ps.tile([P, N], F32, name="wsum", tag="sum2")
        for b in range(BLOCKS):
            for i in range(2):
                nc.scalar.activation(dhalf(root[b], i), spread[i][:], ACT.Relu, bias=1.3, scale=bands[:, b : b + 1])
            if b == 1:
                nc.scalar.copy(*weave(1))
            wt.append(sb.tile([P, D, V], F32, name="wt%d" % b, tag=("wt0", "raw1")[b], align_bytes=64))
            for i in range(2):
                nc.scalar.activation(dhalf(wt[b], i), dhalf(root[b], i), ACT.Square)
        nc.vector.tensor_copy(picked_words[0][:], table_words[:].bitcast(U32).indirect(lst(0)))
        nc.vector.tensor_copy(*weave(0))
        quantize(0)
        picked_words.append(sb.tile([P, HALF], U32, name="picked_words1", tag="grouped0", align_bytes=64))
        nc.vector.tensor_copy(picked_words[1][:], table_words[:].bitcast(U32).indirect(lst(1)))

        def product(i, b, h, slot):
            bank = ps.tile([P, HALF], F32, name="bank", tag="mm%d" % slot)
            cols = slice(P * b, P * (b + 1))
            nc.tensor.matmul_mx(out=bank[:], lhsT=codes[i][:, cols].bitcast(FP8X4), lhsT_scale=scales[i][:, cols],
                                rhs=picked_words[h][:].bitcast(FP8X4), rhs_scale=picked_scales[h][:], start=True, stop=True)
            return bank[:].rearrange("p (v d) -> p d v", d=D)

        def inverse_form(src, shift, name):
            rs, r, f = small(name + "_rs"), small(name + "_r"), small(name + "_f")
            nc.scalar.activation(rs[:], src, ACT.Abs_reciprocal_sqrt, bias=shift)
            nc.scalar.activation(r[:], rs[:], ACT.Square)
            nc.scalar.activation(f[:], r[:], ACT.Square)
            return f

        def squares(dst, src):
            for i in range(2):
                nc.scalar.activation(dhalf(dst, i), dhalf(src, i), ACT.Square)

        def mul(dst, bank, factor, h):
            nc.vector.tensor_tensor(half(dst, h), bank, half(factor, h), ALU.mult)

        uu, u = wide("uu"), wide("u")
        t, wy, tt, ut = wide("t"), wide("wy"), wide("tt"), wide("ut")
        def both(name, in0, in1, op):
            res = small(name)
            nc.vector.tensor_tensor(res[:], in0, in1, op)
            return res

        def shifted(name, src, shift, r2):
            res = small(name)
            nc.vector.scalar_tensor_tensor(res[:], src, shift, r2[:], ALU.add, ALU.mult)
            return res

        def pool_mul(dst, in0, in1):
            nc.gpsimd.tensor_tensor(dst, in0, in1, ALU.mult)

        dsum(third[:, 0:P], wt[0])
        x00, x10 = product(0, 0, 0, 0), product(0, 1, 0, 1)
        x01, x11 = product(0, 0, 1, 2), product(0, 1, 1, 3)
        quantize(1)
        wx = [sb.tile([P, D, V], F32, name="wx%d" % b, tag=("grouped1", "wx1")[b], align_bytes=64) for b in range(BLOCKS)]
        dsum(third[:, P:N], wt[1])
        sum_x = ps.tile([P, 2, N], F32, name="sum_x", tag="sum0")
        sum_y = ps.tile([P, N], F32, name="sum_y", tag="sum1")
        sum_yy = ps.tile([P, N], F32, name="sum_yy", tag="mm4")
        for h, bank in enumerate((x00, x01)):
            mul(u[0], bank, root[0], h)
            pool_mul(half(wx[0], h), half(u[0], h), half(root[0], h))
        y00 = product(1, 0, 0, 0)
        squares(uu[0], u[0])
        mul(u[1], x10, root[1], 0)
        mul(u[1], x11, root[1], 1)
        centre_r2 = inverse_form(third[:], 0.2, "centre")
        squares(uu[1], u[1])
        mul(wx[1], x10, wt[1], 0)
        y01 = product(1, 0, 1, 2)
        dsum(sum_x[:, 1, 0:P], uu[0])
        mul(wx[1], x11, wt[1], 1)
        dsum(sum_x[:, 0, P:N], wx[1])
        mul(t[0], y00, root[0], 0)
        pool_mul(half(wy[0], 0), half(t[0], 0), half(root[0], 0))
        y10 = product(1, 1, 0, 1)
        dsum(sum_x[:, 1, P:N], uu[1])
        dsum(sum_x[:, 0, 0:P], wx[0])
        mul(t[0], y01, root[0], 1)
        for i in range(2):
            pool_mul(dhalf(ut[0], i), dhalf(u[0], i), dhalf(t[0], i))
        squares(tt[0], t[0])
        mul(wy[0], y01, wt[0], 1)
        y11 = product(1, 1, 1, 2)
        centre = shifted("centre", third[:], 0.4, centre_r2)
        sum_xy = ps.tile([P, N], F32, name="sum_xy", tag="sum2")
        dsum(sum_yy[:, 0:P], tt[0])
        dsum(sum_y[:, 0:P], wy[0])
        mul(t[1], y10, root[1], 0)
        pool_mul(half(ut[1], 0), half(u[1], 0), half(t[1], 0))
        csx = both("csx", sum_x[:, 0, :], centre[:], ALU.mult)
        mul(wy[1], y10, wt[1], 0)
        csxx = both("csxx", sum_x[:, 0, :], csx[:], ALU.mult)
        mul(wy[1], y11, wt[1], 1)
        den = both("den", sum_x[:, 1, :], csxx[:], ALU.subtract)
        gain_r2 = inverse_form(den[:], 0.3, "gain")
        mul(t[1], y11, root[1], 1)
        squares(tt[1], t[1])
        dsum(sum_y[:, P:N], wy[1])
        dsum(sum_xy[:, 0:P], ut[0])
        for i in range(2):
            nc.vector.tensor_tensor(half(dhalf(ut[1], i), 1), y11[:, 4 * i : 4 * (i + 1), :], half(dhalf(wx[1], i), 1), ALU.mult)
        dsum(sum_xy[:, P:N], ut[1])
        csxy = both("csxy", sum_y[:], csx[:], ALU.mult)
        sy2 = small("sy2")
        nc.scalar.activation(sy2[:], sum_y[:], ACT.Square)
        dsum(sum_yy[:, P:N], tt[1])
        nsyy = small("nsyy")
        nc.scalar.activation(nsyy[:], sum_yy[:], ACT.Copy, scale=-1.0)
        gain = shifted("gain", den[:], 0.6, gain_r2)
        xy = both("xy", sum_xy[:], csxy[:], ALU.subtract)
        csyy = both("csyy", sy2[:], centre[:], ALU.mult)
        kxy = both("kxy", xy[:], gain[:], ALU.mult)
        fit = both("fit", kxy[:], xy[:], ALU.mult)
        turned = [ps.tile([P, V], F32, name="turned%d" % b, tag="mm%d" % (0, 2)[b]) for b in range(BLOCKS)]
        res = [sb.tile([P, V], F32, name="res%d" % b) for b in range(BLOCKS)]
        parts = [[nsyy[:, 0:P], csyy[:, 0:P], fit[:, 0:P]], [nsyy[:, P:N], csyy[:, P:N], fit[:, P:N]]]
        for last in (False, True):
            for b in range(BLOCKS):
                for i, part in enumerate(parts[b]):
                    if (i == len(parts[b]) - 1) == last:
                        nc.tensor.matmul(turned[b][:], lhsT=part, rhs=ident[:], start=(i == 0), stop=last, is_transpose=True)
        nc.scalar.activation(res[0][:], turned[0][:], ACT.Copy, scale=-1.0)
        nc.scalar.dma_start(out[0:P, :], res[0][:])
        nc.vector.tensor_scalar(res[1][:], turned[1][:], -1.0, None, ALU.mult)
        nc.sync.dma_start(out[P:N, :], res[1][:])
